import numpy as np
import ml_dtypes


def mxq(x, axis, fmt="e4m3"):
    dtype, down = {"e4m3": (ml_dtypes.float8_e4m3fn, 7), "e5m2": (ml_dtypes.float8_e5m2, 14)}[fmt]
    v = np.moveaxis(np.asarray(x, np.float32).astype(ml_dtypes.bfloat16).astype(np.float64), axis, -1)
    blocks = v.reshape(v.shape[:-1] + (-1, 32))
    amax = np.abs(blocks).max(-1, keepdims=True)
    byte = np.maximum(np.where(amax > 0, np.frexp(amax)[1] - 1 + 127, 0) - down, 1)
    scale = np.exp2(byte - 127.0)
    codes = (blocks / scale).astype(np.float32).astype(dtype).astype(np.float64)
    return np.moveaxis((codes * scale).reshape(v.shape), -1, axis)


WIDE = False


def mx_kscale(k):
    if not WIDE:
        return np.ones(k)
    levels = np.array([10, -10, 5, -5, 0])
    if k % 512:
        return np.exp2(np.random.permutation(np.resize(levels, k // 32))).repeat(32)
    a = np.empty((k // 512, 16))
    for p in range(k // 512):
        a[p, :8] = np.random.permutation(np.resize(levels, 8))
        for g in range(8):
            far = levels[np.abs(levels - a[p, g]) >= 10]
            a[p, g + 8] = far[np.random.randint(len(far))]
    return np.exp2(a.ravel()).repeat(32)


def f64(x):
    return np.asarray(x).astype(np.float64)


def striped(idx):
    return np.tile(idx.reshape(-1, 16).T, (8, 1)).astype(np.uint16)


def unstriped(offs):
    return offs[:16].T.reshape(-1).astype(np.int64)


def pack_weight(w):
    k, n = w.shape
    w = f64(np.asarray(w, np.float32).astype(ml_dtypes.bfloat16)).reshape(k // 32, 32, n)
    amax = np.abs(w).max(1)
    byte = np.clip(np.where(amax > 0, np.frexp(amax)[1] - 1 + 127 - 7, 1), 1, 254)
    scaled = (w * np.exp2(127.0 - byte)[:, None, :]).reshape(k, n).astype(np.float32)
    words = np.ascontiguousarray(scaled.reshape(k // 512, 128, 4, n).transpose(0, 1, 3, 2)).astype(ml_dtypes.float8_e4m3fn).view(np.uint8)
    return words, np.ascontiguousarray(byte.astype(np.uint8).reshape(k // 512, 16, n))


def unpack_weight(words, scales):
    g, p, n, _ = words.shape
    vals = np.ascontiguousarray(words).view(ml_dtypes.float8_e4m3fn).astype(np.float64) * np.repeat(np.exp2(scales.astype(np.float64) - 127.0), 8, axis=1)[..., None]
    return vals.transpose(0, 1, 3, 2).reshape(g * 512, n)


def relu(v):
    return np.maximum(v, 0.0)


K, T, S, D, N, H, V, U = 1024, 2048, 1024, 4, 128, 512, 256, 512


def setup_inputs():
    n = np.random.standard_normal
    s = mx_kscale(K)[:, None]
    u = mx_kscale(H)
    packed_xT = pack_weight(n((K, T)) * s)
    return {
        "x_words": packed_xT[0],
        "x_scales": packed_xT[1],
        "w1": (n((K, H)) / np.sqrt(K) / s).astype(np.float32),
        "dist": (np.random.uniform(0.1, 1.2, (H, S))).astype(np.float32),
        "brdf": (np.random.uniform(0.2, 1.2, (H, U))).astype(np.float32),
        "unit": (np.random.uniform(0.6, 1.4, (H, 1)) * u[:, None]).astype(np.float32),
        "w2": (n((H, N)) / np.sqrt(H) / u[:, None]).astype(np.float32),
        "offs": striped(np.random.permutation(T)[:S]),
        "pix": striped(np.random.permutation(np.concatenate([np.arange(V), np.random.randint(0, V, U - V)]))),
    }


def reference(x_words, x_scales, w1, dist, brdf, unit, w2, offs, pix):
    xq = unpack_weight(x_words, x_scales)[:, unstriped(offs)]
    y = mxq(f64(w1), 0, "e4m3").T @ xq
    flux = np.log(np.exp(y) + 1.0)
    cone = relu(-1.0 * f64(dist) + 1.0)
    fw = flux * cone
    num = fw.reshape(len(fw), -1, D).sum(axis=2)
    rad = f64(dist).reshape(len(f64(dist)), -1, D).max(axis=2)
    est = num / ((rad) ** 2 + 0.2)
    ep = est[:, unstriped(pix)]
    rad2 = ep * f64(brdf)
    hid = f64(unit) * rad2
    return mxq(f64(w2), 0, "e4m3").T @ mxq(hid, 0, "e4m3")

@@ -1,0 +1,275 @@
+import math
+from contextlib import ExitStack
+
+import concourse.mybir as mybir
+from concourse.masks import make_identity
+
+K, T, S, D, N, H, V, U = 1024, 2048, 1024, 4, 128, 512, 256, 512
+FLOPS = 2 * K * H * S + 2 * H * N * U
+
+F32 = mybir.dt.float32
+BF16 = mybir.dt.bfloat16
+I32 = mybir.dt.int32
+U32 = mybir.dt.uint32
+U16 = mybir.dt.uint16
+U8 = mybir.dt.uint8
+FP8X4 = mybir.dt.float8_e4m3fn_x4
+ALU = mybir.AluOpType
+ACT = mybir.ActivationFunctionType
+AX = mybir.AxisListType
+
+P = 128
+PACK = 4
+PASSES = K // (P * PACK)
+HALF = 512
+HALVES = S // HALF
+PIX_HALF = U // 2
+TINY = 2.0 ** -60
+
+
+def tile_picked_yphotn_lin_p_kernel(
+    tc, x_words, x_scales, w1, dist, brdf, unit, w2, offs, pix, out
+):
+    nc = tc.nc
+    with ExitStack() as ctx:
+        lists = ctx.enter_context(tc.tile_pool(name="lists", bufs=1))
+        sb = ctx.enter_context(tc.tile_pool(name="sb", bufs=1))
+        psum = ctx.enter_context(tc.psum_pool(name="psum", bufs=1))
+
+        def tile(name, shape, dtype):
+            return sb.tile(shape, dtype, name=name, align_bytes=64)
+
+        offs_sb = lists.tile([P, S // 16], U16, name="offs_sb")
+        pix_sb = lists.tile([P, U // 16], U16, name="pix_sb")
+
+        x_sb = [tile(f"x_sb{o}", [P, T], U32) for o in range(PASSES)]
+        xs_sb = tile("xs_sb", [P, T], U8)
+        w1_sb = [tile(f"w1_sb{o}", [P, PACK, H], F32) for o in range(PASSES)]
+        dist_sb = [tile(f"dist_sb{t}", [P, S], F32) for t in range(PACK)]
+        brdf_sb = tile("brdf_sb", [P, PACK, U], F32)
+        w2_sb = tile("w2_sb", [P, PACK, N], F32)
+        unit_sb = tile("unit_sb", [P, PACK], F32)
+
+        def load_words(o):
+            nc.sync.dma_start(
+                out=x_sb[o][:].bitcast(I32),
+                in_=x_words[o].rearrange("p n t -> p (n t)").bitcast(I32),
+            )
+
+        nc.sync.dma_start(offs_sb[:], offs)
+        load_words(0)
+        nc.vector.memset(xs_sb[:].bitcast(I32), 0)
+        for q in range(4):
+            nc.sync.dma_start(
+                out=xs_sb[32 * q : 32 * q + 4 * PASSES, :].bitcast(I32),
+                in_=x_scales[:, 4 * q : 4 * q + 4, :].bitcast(I32),
+            )
+        for o in range(PASSES):
+            nc.sync.dma_start(
+                out=w1_sb[o][:],
+                in_=w1[512 * o : 512 * (o + 1), :].rearrange("(p j) c -> p j c", j=PACK),
+            )
+        load_words(1)
+        dist_rows = dist.rearrange("(p t) s -> p t s", t=PACK)
+        for t in range(PACK):
+            nc.sync.dma_start(out=dist_sb[t][:], in_=dist_rows[:, t, :])
+        nc.sync.dma_start(out=w2_sb[:], in_=w2.rearrange("(p t) n -> p t n", t=PACK))
+        nc.sync.dma_start(out=unit_sb[:], in_=unit.rearrange("(p t) o -> p (t o)", t=PACK))
+        nc.sync.dma_start(pix_sb[:], pix)
+        nc.sync.dma_start(out=brdf_sb[:], in_=brdf.rearrange("(p t) r -> p t r", t=PACK))
+
+        xg = [[tile(f"xg{o}{h}", [P, HALF], U32) for h in range(HALVES)] for o in range(PASSES)]
+        sg = [tile(f"sg{h}", [P, HALF], U8) for h in range(HALVES)]
+        w1_bf = [tile(f"w1_bf{o}", [P, PACK * H], BF16) for o in range(PASSES)]
+        w1_q = [tile(f"w1_q{o}", [P, H], U32) for o in range(PASSES)]
+        w1_s = [tile(f"w1_s{o}", [P, H], U8) for o in range(PASSES)]
+
+        def offs_half(h):
+            return offs_sb[:, h * (HALF // 16) : (h + 1) * (HALF // 16)]
+
+        def gather_words(o, h):
+            nc.vector.tensor_copy(xg[o][h][:], x_sb[o][:].indirect(offs_half(h)))
+
+        def gather_scales(h):
+            nc.vector.tensor_copy(sg[h][:], xs_sb[:].indirect(offs_half(h)))
+
+        def w1_views(o, m0, m1):
+            dst = w1_bf[o][:].rearrange("p (t m j) -> p m j t", t=PACK, j=PACK)[:, m0:m1]
+            src = w1_sb[o][:].rearrange("p j (m t) -> p m j t", t=PACK)[:, m0:m1]
+            return dst, src
+
+        def quantize_w1(o):
+            nc.vector.quantize_mx(out=w1_q[o][:].bitcast(FP8X4), scales=w1_s[o][:], in_=w1_bf[o][:])
+
+        for h in range(HALVES):
+            gather_words(0, h)
+        dst, src = w1_views(0, 0, P)
+        nc.scalar.copy(dst, src)
+        for h in range(HALVES):
+            gather_scales(h)
+        dst, src = w1_views(1, 0, P)
+        nc.scalar.copy(dst, src)
+        quantize_w1(0)
+        gather_words(1, 0)
+        quantize_w1(1)
+        gather_words(1, 1)
+
+        y = [[psum.tile([P, HALF], F32, name=f"y{t}{h}", tag=f"bank{t}{h}") for h in range(HALVES)] for t in range(PACK)]
+        sig = [tile(f"sig{t}", [P, S], F32) for t in range(PACK)]
+
+        def by_d(tl, h):
+            return tl[:, h * HALF : (h + 1) * HALF].rearrange("p (d v) -> p d v", d=D)
+
+        def y_by_d(t, h):
+            return y[t][h][:].rearrange("p (v d) -> p d v", d=D)
+
+        for h in range(HALVES):
+            for t in range(PACK):
+                cols = slice(P * t, P * (t + 1))
+                for o in range(PASSES):
+                    nc.tensor.matmul_mx(
+                        out=y[t][h][:],
+                        lhsT=w1_q[o][:, cols].bitcast(FP8X4),
+                        lhsT_scale=w1_s[o][:, cols],
+                        rhs=xg[o][h][:].bitcast(FP8X4),
+                        rhs_scale=sg[h][4 * o : P, :],
+                        start=(o == 0),
+                        stop=(o == PASSES - 1),
+                    )
+                nc.scalar.activation(by_d(sig[t], h), y_by_d(t, h), ACT.Sigmoid, scale=-1.0)
+
+        rad = tile("rad", [P, PACK, V], F32)
+        arad = tile("arad", [P, PACK * V], F32)
+        ncone = [tile(f"ncone{t}", [P, S], F32) for t in range(PACK)]
+        for t in range(PACK):
+            nc.vector.tensor_reduce(rad[:, t, :], dist_sb[t][:].rearrange("p (v d) -> p v d", d=D), AX.X, ALU.max)
+            nc.gpsimd.tensor_scalar(
+                ncone[t][:].rearrange("p (h d v) -> p h d v", h=HALVES, d=D),
+                dist_sb[t][:].rearrange("p (h v d) -> p h d v", h=HALVES, d=D),
+                -1.0, 1.0, ALU.mult, ALU.add,
+            )
+            nc.vector.scalar_tensor_tensor(
+                arad[:, t * V : (t + 1) * V], rad[:, t, :], -1.0, rad[:, t, :], ALU.mult, ALU.max
+            )
+        w2_bf = tile("w2_bf", [P, N * PACK], BF16)
+        w2_q = tile("w2_q", [P, N], U32)
+        w2_s = tile("w2_s", [P, N], U8)
+        nc.vector.tensor_copy(
+            w2_bf[:].rearrange("p (c i t) -> p c t i", i=4, t=PACK),
+            w2_sb[:].rearrange("p t (c i) -> p c t i", i=4),
+        )
+        nc.vector.quantize_mx(out=w2_q[:].bitcast(FP8X4), scales=w2_s[:], in_=w2_bf[:])
+        unit5 = tile("unit5", [P, PACK], F32)
+        nc.gpsimd.tensor_scalar(unit5[:], unit_sb[:], -5.0, 0.0, ALU.mult, ALU.add)
+
+        ident = tile("ident", [P, P], F32)
+        make_identity(nc, ident[:])
+
+        lsig = [tile(f"lsig{t}", [P, S], F32) for t in range(PACK)]
+        lrad = tile("lrad", [P, PACK * V], F32)
+        est = [tile(f"est{t}", [P, 2 * V], F32) for t in range(PACK)]
+        nflux = [tile(f"nflux{t}", [P, S], F32) for t in range(PACK)]
+        fw = [tile(f"fw{t}", [P, S], F32) for t in range(PACK)]
+        numt = [tile(f"numt{t}", [P, V], F32) for t in range(PACK - 1)]
+        pairs = tile("pairs", [P, HALVES, 2 * P], F32)
+        num_last = tile("num_last", [P, V], F32)
+        ep = [tile(f"ep{t}", [P, U], F32) for t in range(PACK)]
+        hid = tile("hid", [P, PACK, U], F32)
+        LAST = PACK - 1
+
+        def weigh(t):
+            for h in range(HALVES):
+                nc.vector.scalar_tensor_tensor(
+                    by_d(nflux[t], h), y_by_d(t, h), -1.0, by_d(lsig[t], h), ALU.mult, ALU.min
+                )
+            nc.vector.scalar_tensor_tensor(fw[t][:], ncone[t][:], 0.0, nflux[t][:], ALU.max, ALU.mult)
+
+        def sum_on_tensor(t):
+            turned = psum.tile([P, HALF], F32, name=f"turned{t}", tag=f"bank{t}0")
+            for h in range(HALVES):
+                for d in range(D):
+                    c0 = h * HALF + d * P
+                    nc.tensor.matmul(
+                        turned[:, h * P : (h + 1) * P], fw[t][:, c0 : c0 + P], ident[:],
+                        start=(d == 0), stop=(d == D - 1), is_transpose=True,
+                    )
+            nc.scalar.copy(numt[t][:], turned[:, :V])
+            back = psum.tile([P, HALF], F32, name=f"back{t}", tag=f"bank{t}1")
+            for h in range(HALVES):
+                nc.tensor.transpose(back[:, h * P : (h + 1) * P], numt[t][:, h * P : (h + 1) * P], ident[:])
+            return back[:, :V]
+
+        def sum_on_vector(t):
+            four = fw[t][:].rearrange("p (h e w) -> p h e w", h=HALVES, e=2)
+            nc.vector.tensor_tensor(pairs[:], four[:, :, 0, :], four[:, :, 1, :], ALU.add)
+            nc.vector.tensor_tensor(
+                num_last[:].rearrange("p (h v) -> p h v", h=HALVES), pairs[:, :, :P], pairs[:, :, P:], ALU.add
+            )
+            return num_last[:]
+
+        def estimate(t, num):
+            nc.vector.scalar_tensor_tensor(est[t][:, :V], num, unit5[:, t : t + 1], est[t][:, V:], ALU.mult, ALU.mult)
+
+        def pix_half(g):
+            return pix_sb[:, g * (PIX_HALF // 16) : (g + 1) * (PIX_HALF // 16)]
+
+        def fetch(t, g):
+            cols = slice(g * PIX_HALF, (g + 1) * PIX_HALF)
+            nc.scalar.activation(ep[t][:, cols], est[t][:].indirect(pix_half(g)), ACT.Copy)
+
+        for t in range(PACK):
+            nc.scalar.activation(lsig[t][:], sig[t][:], ACT.Ln, bias=TINY)
+        nc.scalar.activation(lrad[:], arad[:], ACT.Ln, bias=TINY)
+        nums = []
+        for t in range(2):
+            weigh(t)
+            nums.append(sum_on_tensor(t))
+        for t in range(PACK):
+            nc.scalar.activation(
+                est[t][:, V:], lrad[:, t * V : (t + 1) * V], ACT.Sigmoid, scale=-2.0, bias=-math.log(5.0)
+            )
+        weigh(2)
+        nums.append(sum_on_tensor(2))
+        for t in range(2):
+            estimate(t, nums[t])
+            for g in range(2):
+                fetch(t, g)
+            nc.gpsimd.tensor_tensor(hid[:, t, :], ep[t][:], brdf_sb[:, t, :], ALU.mult)
+        weigh(LAST)
+        estimate(2, nums[2])
+        for g in range(2):
+            fetch(2, g)
+        nc.gpsimd.tensor_tensor(hid[:, 2, :], ep[2][:], brdf_sb[:, 2, :], ALU.mult)
+        estimate(LAST, sum_on_vector(LAST))
+        fetch(LAST, 1)
+        nc.vector.tensor_tensor(
+            hid[:, LAST, :PIX_HALF], est[LAST][:].indirect(pix_half(0)), brdf_sb[:, LAST, :PIX_HALF], ALU.mult
+        )
+
+        hid_bf = [tile(f"hid_bf{g}", [P, PIX_HALF * PACK], BF16) for g in range(2)]
+        hid_q = [tile(f"hid_q{g}", [P, PIX_HALF], U32) for g in range(2)]
+        hid_s = [tile(f"hid_s{g}", [P, PIX_HALF], U8) for g in range(2)]
+        res = [tile(f"res{g}", [P, PIX_HALF], F32) for g in range(2)]
+        for g in range(2):
+            cols = slice(g * PIX_HALF, (g + 1) * PIX_HALF)
+            if g == 1:
+                nc.vector.tensor_tensor(hid[:, LAST, cols], ep[LAST][:, cols], brdf_sb[:, LAST, cols], ALU.mult)
+            nc.vector.tensor_copy(
+                hid_bf[g][:].rearrange("p (c i t) -> p c t i", i=4, t=PACK),
+                hid[:, :, cols].rearrange("p t (c i) -> p c t i", i=4),
+            )
+        for g in range(2):
+            cols = slice(g * PIX_HALF, (g + 1) * PIX_HALF)
+            nc.vector.quantize_mx(out=hid_q[g][:].bitcast(FP8X4), scales=hid_s[g][:], in_=hid_bf[g][:])
+            acc = psum.tile([P, HALF], F32, name=f"acc{g}", tag=f"bank0{g}")
+            nc.tensor.matmul_mx(
+                out=acc[:, :PIX_HALF],
+                lhsT=w2_q[:].bitcast(FP8X4),
+                lhsT_scale=w2_s[:],
+                rhs=hid_q[g][:].bitcast(FP8X4),
+                rhs_scale=hid_s[g][:],
+                start=True,
+                stop=True,
+            )
+            nc.scalar.copy(res[g][:], acc[:, :PIX_HALF])
+            nc.sync.dma_start(out=out[:, cols], in_=res[g][:])

@@ -25,6 +25,8 @@ HALF = 512
 HALVES = S // HALF
 PIX_HALF = U // 2
 TINY = 2.0 ** -60
+CAST_SPLIT = 48
+PIX_PIECES = ((0, 256), (256, 384), (384, 512))
 
 
 def tile_picked_yphotn_lin_p_kernel(
@@ -36,8 +38,8 @@ def tile_picked_yphotn_lin_p_kernel(
         sb = ctx.enter_context(tc.tile_pool(name="sb", bufs=1))
         psum = ctx.enter_context(tc.psum_pool(name="psum", bufs=1))
 
-        def tile(name, shape, dtype):
-            return sb.tile(shape, dtype, name=name, align_bytes=64)
+        def tile(name, shape, dtype, tag=None):
+            return sb.tile(shape, dtype, name=name, tag=tag or name, align_bytes=64)
 
         offs_sb = lists.tile([P, S // 16], U16, name="offs_sb")
         pix_sb = lists.tile([P, U // 16], U16, name="pix_sb")
@@ -56,11 +58,11 @@ def tile_picked_yphotn_lin_p_kernel(
                 in_=x_words[o].rearrange("p n t -> p (n t)").bitcast(I32),
             )
 
-        nc.sync.dma_start(offs_sb[:], offs)
         load_words(0)
-        nc.vector.memset(xs_sb[:].bitcast(I32), 0)
+        nc.sync.dma_start(offs_sb[:], offs)
+        nc.gpsimd.memset(xs_sb[:].bitcast(I32), 0)
         for q in range(4):
-            nc.sync.dma_start(
+            nc.gpsimd.dma_start(
                 out=xs_sb[32 * q : 32 * q + 4 * PASSES, :].bitcast(I32),
                 in_=x_scales[:, 4 * q : 4 * q + 4, :].bitcast(I32),
             )
@@ -78,7 +80,13 @@ def tile_picked_yphotn_lin_p_kernel(
         nc.sync.dma_start(pix_sb[:], pix)
         nc.sync.dma_start(out=brdf_sb[:], in_=brdf.rearrange("(p t) r -> p t r", t=PACK))
 
-        xg = [[tile(f"xg{o}{h}", [P, HALF], U32) for h in range(HALVES)] for o in range(PASSES)]
+        ident = tile("ident", [P, P], F32)
+        make_identity(nc, ident[:])
+        warm = tile("warm", [P, 2], F32)
+        nc.vector.memset(warm[:, 0:1], 0.0)
+        nc.scalar.activation(warm[:, 1:2], warm[:, 0:1], ACT.Sigmoid)
+
+        xg = {}
         sg = [tile(f"sg{h}", [P, HALF], U8) for h in range(HALVES)]
         w1_bf = [tile(f"w1_bf{o}", [P, PACK * H], BF16) for o in range(PASSES)]
         w1_q = [tile(f"w1_q{o}", [P, H], U32) for o in range(PASSES)]
@@ -87,15 +95,16 @@ def tile_picked_yphotn_lin_p_kernel(
         def offs_half(h):
             return offs_sb[:, h * (HALF // 16) : (h + 1) * (HALF // 16)]
 
-        def gather_words(o, h):
-            nc.vector.tensor_copy(xg[o][h][:], x_sb[o][:].indirect(offs_half(h)))
+        def gather_words(o, h, tag=None):
+            xg[o, h] = tile(f"xg{o}{h}", [P, HALF], U32, tag)
+            nc.vector.tensor_copy(xg[o, h][:], x_sb[o][:].indirect(offs_half(h)))
 
         def gather_scales(h):
             nc.vector.tensor_copy(sg[h][:], xs_sb[:].indirect(offs_half(h)))
 
         def w1_views(o, m0, m1):
-            dst = w1_bf[o][:].rearrange("p (t m j) -> p m j t", t=PACK, j=PACK)[:, m0:m1]
-            src = w1_sb[o][:].rearrange("p j (m t) -> p m j t", t=PACK)[:, m0:m1]
+            dst = w1_bf[o][:].rearrange("p (t m j) -> p m t j", t=PACK, j=PACK)[:, m0:m1]
+            src = w1_sb[o][:].rearrange("p j (m t) -> p m t j", t=PACK)[:, m0:m1]
             return dst, src
 
         def quantize_w1(o):
@@ -107,21 +116,20 @@ def tile_picked_yphotn_lin_p_kernel(
         nc.scalar.copy(dst, src)
         for h in range(HALVES):
             gather_scales(h)
-        dst, src = w1_views(1, 0, P)
+        dst, src = w1_views(1, 0, CAST_SPLIT)
         nc.scalar.copy(dst, src)
+        dst, src = w1_views(1, CAST_SPLIT, P)
+        nc.vector.tensor_copy(dst, src)
         quantize_w1(0)
-        gather_words(1, 0)
         quantize_w1(1)
+        gather_words(1, 0, "xs_sb")
         gather_words(1, 1)
 
         y = [[psum.tile([P, HALF], F32, name=f"y{t}{h}", tag=f"bank{t}{h}") for h in range(HALVES)] for t in range(PACK)]
         sig = [tile(f"sig{t}", [P, S], F32) for t in range(PACK)]
 
-        def by_d(tl, h):
-            return tl[:, h * HALF : (h + 1) * HALF].rearrange("p (d v) -> p d v", d=D)
-
-        def y_by_d(t, h):
-            return y[t][h][:].rearrange("p (v d) -> p d v", d=D)
+        def half(tl, h):
+            return tl[:, h * HALF : (h + 1) * HALF]
 
         for h in range(HALVES):
             for t in range(PACK):
@@ -131,145 +139,164 @@ def tile_picked_yphotn_lin_p_kernel(
                         out=y[t][h][:],
                         lhsT=w1_q[o][:, cols].bitcast(FP8X4),
                         lhsT_scale=w1_s[o][:, cols],
-                        rhs=xg[o][h][:].bitcast(FP8X4),
+                        rhs=xg[o, h][:].bitcast(FP8X4),
                         rhs_scale=sg[h][4 * o : P, :],
                         start=(o == 0),
                         stop=(o == PASSES - 1),
                     )
-                nc.scalar.activation(by_d(sig[t], h), y_by_d(t, h), ACT.Sigmoid, scale=-1.0)
+                nc.scalar.activation(half(sig[t], h), y[t][h][:], ACT.Sigmoid, scale=-1.0)
 
-        rad = tile("rad", [P, PACK, V], F32)
+        rad = tile("rad", [P, PACK, V], F32, "x_sb1")
         arad = tile("arad", [P, PACK * V], F32)
         ncone = [tile(f"ncone{t}", [P, S], F32) for t in range(PACK)]
         for t in range(PACK):
             nc.vector.tensor_reduce(rad[:, t, :], dist_sb[t][:].rearrange("p (v d) -> p v d", d=D), AX.X, ALU.max)
-            nc.gpsimd.tensor_scalar(
-                ncone[t][:].rearrange("p (h d v) -> p h d v", h=HALVES, d=D),
-                dist_sb[t][:].rearrange("p (h v d) -> p h d v", h=HALVES, d=D),
-                -1.0, 1.0, ALU.mult, ALU.add,
-            )
-            nc.vector.scalar_tensor_tensor(
-                arad[:, t * V : (t + 1) * V], rad[:, t, :], -1.0, rad[:, t, :], ALU.mult, ALU.max
-            )
+            nc.gpsimd.tensor_scalar(ncone[t][:], dist_sb[t][:], -1.0, 1.0, ALU.mult, ALU.add)
+        rad_flat = rad[:].rearrange("p t v -> p (t v)")
+        nc.vector.scalar_tensor_tensor(arad[:], rad_flat, -1.0, rad_flat, ALU.mult, ALU.max)
         w2_bf = tile("w2_bf", [P, N * PACK], BF16)
         w2_q = tile("w2_q", [P, N], U32)
         w2_s = tile("w2_s", [P, N], U8)
         nc.vector.tensor_copy(
-            w2_bf[:].rearrange("p (c i t) -> p c t i", i=4, t=PACK),
-            w2_sb[:].rearrange("p t (c i) -> p c t i", i=4),
+            w2_bf[:].rearrange("p (c i t) -> p c t i", i=2, t=PACK),
+            w2_sb[:].rearrange("p t (c i) -> p c t i", i=2),
         )
         nc.vector.quantize_mx(out=w2_q[:].bitcast(FP8X4), scales=w2_s[:], in_=w2_bf[:])
         unit5 = tile("unit5", [P, PACK], F32)
         nc.gpsimd.tensor_scalar(unit5[:], unit_sb[:], -5.0, 0.0, ALU.mult, ALU.add)
 
-        ident = tile("ident", [P, P], F32)
-        make_identity(nc, ident[:])
-
         lsig = [tile(f"lsig{t}", [P, S], F32) for t in range(PACK)]
         lrad = tile("lrad", [P, PACK * V], F32)
         est = [tile(f"est{t}", [P, 2 * V], F32) for t in range(PACK)]
         nflux = [tile(f"nflux{t}", [P, S], F32) for t in range(PACK)]
-        fw = [tile(f"fw{t}", [P, S], F32) for t in range(PACK)]
-        numt = [tile(f"numt{t}", [P, V], F32) for t in range(PACK - 1)]
-        pairs = tile("pairs", [P, HALVES, 2 * P], F32)
-        num_last = tile("num_last", [P, V], F32)
-        ep = [tile(f"ep{t}", [P, U], F32) for t in range(PACK)]
-        hid = tile("hid", [P, PACK, U], F32)
+        fw = [tile(f"fw{t}", [P, 2, S // 2], F32) for t in range(PACK)]
+        recip = tile("recip", [P, PACK * V], F32)
+        ep = [tile(f"ep{g}", [P, PACK, PIX_HALF], F32) for g in range(2)]
         LAST = PACK - 1
 
-        def weigh(t):
+        def clamp(t):
             for h in range(HALVES):
-                nc.vector.scalar_tensor_tensor(
-                    by_d(nflux[t], h), y_by_d(t, h), -1.0, by_d(lsig[t], h), ALU.mult, ALU.min
-                )
-            nc.vector.scalar_tensor_tensor(fw[t][:], ncone[t][:], 0.0, nflux[t][:], ALU.max, ALU.mult)
+                nc.vector.scalar_tensor_tensor(half(nflux[t], h), y[t][h][:], -1.0, half(lsig[t], h), ALU.mult, ALU.min)
+
+        def weigh(t):
+            clamp(t)
+            for h in range(HALVES):
+                for e in range(2):
+                    nc.vector.scalar_tensor_tensor(
+                        fw[t][:, e, 2 * P * h : 2 * P * (h + 1)].rearrange("p (v d) -> p v d", d=2),
+                        half(ncone[t], h).rearrange("p (v e d) -> p v e d", e=2, d=2)[:, :, e, :],
+                        0.0,
+                        half(nflux[t], h).rearrange("p (v e d) -> p v e d", e=2, d=2)[:, :, e, :],
+                        ALU.max,
+                        ALU.mult,
+                    )
 
         def sum_on_tensor(t):
             turned = psum.tile([P, HALF], F32, name=f"turned{t}", tag=f"bank{t}0")
             for h in range(HALVES):
                 for d in range(D):
-                    c0 = h * HALF + d * P
+                    c0 = 2 * P * h + d % 2
                     nc.tensor.matmul(
-                        turned[:, h * P : (h + 1) * P], fw[t][:, c0 : c0 + P], ident[:],
+                        turned[:, h * P : (h + 1) * P], fw[t][:, d // 2, c0 : 2 * P * (h + 1) : 2], ident[:],
                         start=(d == 0), stop=(d == D - 1), is_transpose=True,
                     )
-            nc.scalar.copy(numt[t][:], turned[:, :V])
+            nc.scalar.copy(est[t][:, V:], turned[:, :V])
             back = psum.tile([P, HALF], F32, name=f"back{t}", tag=f"bank{t}1")
             for h in range(HALVES):
-                nc.tensor.transpose(back[:, h * P : (h + 1) * P], numt[t][:, h * P : (h + 1) * P], ident[:])
+                nc.tensor.transpose(back[:, h * P : (h + 1) * P], est[t][:, V + h * P : V + (h + 1) * P], ident[:])
             return back[:, :V]
 
-        def sum_on_vector(t):
-            four = fw[t][:].rearrange("p (h e w) -> p h e w", h=HALVES, e=2)
-            nc.vector.tensor_tensor(pairs[:], four[:, :, 0, :], four[:, :, 1, :], ALU.add)
-            nc.vector.tensor_tensor(
-                num_last[:].rearrange("p (h v) -> p h v", h=HALVES), pairs[:, :, :P], pairs[:, :, P:], ALU.add
+        def estimate(t, num, c0, c1):
+            nc.vector.scalar_tensor_tensor(
+                est[t][:, c0:c1], num[:, c0:c1], unit5[:, t : t + 1], recip[:, t * V + c0 : t * V + c1], ALU.mult, ALU.mult
             )
-            return num_last[:]
 
-        def estimate(t, num):
-            nc.vector.scalar_tensor_tensor(est[t][:, :V], num, unit5[:, t : t + 1], est[t][:, V:], ALU.mult, ALU.mult)
+        def looked_up(t, c0, c1):
+            return est[t][:].indirect(pix_sb[:, c0 // 16 : c1 // 16])
 
-        def pix_half(g):
-            return pix_sb[:, g * (PIX_HALF // 16) : (g + 1) * (PIX_HALF // 16)]
+        def fetched(t, c0, c1):
+            g = c0 // PIX_HALF
+            return ep[g][:, t, c0 - g * PIX_HALF : c1 - g * PIX_HALF]
 
-        def fetch(t, g):
-            cols = slice(g * PIX_HALF, (g + 1) * PIX_HALF)
-            nc.scalar.activation(ep[t][:, cols], est[t][:].indirect(pix_half(g)), ACT.Copy)
+        def fetch(t):
+            for c0 in (0, PIX_HALF):
+                nc.scalar.activation(fetched(t, c0, c0 + PIX_HALF), looked_up(t, c0, c0 + PIX_HALF), ACT.Copy)
 
-        for t in range(PACK):
+        for h in range(HALVES):
+            nc.scalar.activation(half(lsig[0], h), half(sig[0], h), ACT.Ln, bias=TINY)
+        for t in range(1, PACK):
             nc.scalar.activation(lsig[t][:], sig[t][:], ACT.Ln, bias=TINY)
         nc.scalar.activation(lrad[:], arad[:], ACT.Ln, bias=TINY)
         nums = []
-        for t in range(2):
-            weigh(t)
-            nums.append(sum_on_tensor(t))
-        for t in range(PACK):
+        weigh(0)
+        nums.append(sum_on_tensor(0))
+        for c0 in (0, 2 * V):
             nc.scalar.activation(
-                est[t][:, V:], lrad[:, t * V : (t + 1) * V], ACT.Sigmoid, scale=-2.0, bias=-math.log(5.0)
+                recip[:, c0 : c0 + 2 * V], lrad[:, c0 : c0 + 2 * V], ACT.Sigmoid, scale=-2.0, bias=-math.log(5.0)
             )
+        weigh(1)
+        nums.append(sum_on_tensor(1))
         weigh(2)
         nums.append(sum_on_tensor(2))
         for t in range(2):
-            estimate(t, nums[t])
-            for g in range(2):
-                fetch(t, g)
-            nc.gpsimd.tensor_tensor(hid[:, t, :], ep[t][:], brdf_sb[:, t, :], ALU.mult)
-        weigh(LAST)
-        estimate(2, nums[2])
-        for g in range(2):
-            fetch(2, g)
-        nc.gpsimd.tensor_tensor(hid[:, 2, :], ep[2][:], brdf_sb[:, 2, :], ALU.mult)
-        estimate(LAST, sum_on_vector(LAST))
-        fetch(LAST, 1)
-        nc.vector.tensor_tensor(
-            hid[:, LAST, :PIX_HALF], est[LAST][:].indirect(pix_half(0)), brdf_sb[:, LAST, :PIX_HALF], ALU.mult
-        )
-
-        hid_bf = [tile(f"hid_bf{g}", [P, PIX_HALF * PACK], BF16) for g in range(2)]
-        hid_q = [tile(f"hid_q{g}", [P, PIX_HALF], U32) for g in range(2)]
-        hid_s = [tile(f"hid_s{g}", [P, PIX_HALF], U8) for g in range(2)]
-        res = [tile(f"res{g}", [P, PIX_HALF], F32) for g in range(2)]
-        for g in range(2):
-            cols = slice(g * PIX_HALF, (g + 1) * PIX_HALF)
-            if g == 1:
-                nc.vector.tensor_tensor(hid[:, LAST, cols], ep[LAST][:, cols], brdf_sb[:, LAST, cols], ALU.mult)
-            nc.vector.tensor_copy(
-                hid_bf[g][:].rearrange("p (c i t) -> p c t i", i=4, t=PACK),
-                hid[:, :, cols].rearrange("p t (c i) -> p c t i", i=4),
+            estimate(t, nums[t], 0, V)
+            fetch(t)
+        clamp(LAST)
+        num_last = est[LAST][:, V:]
+        fw_last = fw[LAST][:].rearrange("p e w -> p (e w)")
+        for h in range(HALVES):
+            nc.vector.scalar_tensor_tensor(
+                fw_last[:, h * HALF : (h + 1) * HALF], half(ncone[LAST], h), 0.0, half(nflux[LAST], h), ALU.max, ALU.mult
             )
-        for g in range(2):
-            cols = slice(g * PIX_HALF, (g + 1) * PIX_HALF)
-            nc.vector.quantize_mx(out=hid_q[g][:].bitcast(FP8X4), scales=hid_s[g][:], in_=hid_bf[g][:])
-            acc = psum.tile([P, HALF], F32, name=f"acc{g}", tag=f"bank0{g}")
+        for h in range(HALVES):
+            nc.vector.tensor_reduce(
+                num_last[:, h * P : (h + 1) * P],
+                fw_last[:, h * HALF : (h + 1) * HALF].rearrange("p (v d) -> p v d", d=D),
+                AX.X,
+                ALU.add,
+            )
+        for h in range(HALVES):
+            estimate(LAST, num_last, h * P, (h + 1) * P)
+        estimate(2, nums[2], 0, V)
+        fetch(2)
+        nc.vector.tensor_copy(fetched(LAST, 0, PIX_HALF), looked_up(LAST, 0, PIX_HALF))
+        nc.vector.tensor_copy(fetched(LAST, PIX_HALF, U), looked_up(LAST, PIX_HALF, U))
+
+        hid_bf = [tile(f"hid_bf{c0}", [P, (c1 - c0) * PACK], BF16) for c0, c1 in PIX_PIECES]
+
+        def shade(g):
+            c0, c1 = PIX_PIECES[g]
+            side = c0 // PIX_HALF
+            nc.vector.tensor_tensor(
+                hid_bf[g][:].rearrange("p (c i t) -> p c t i", i=2, t=PACK),
+                ep[side][:, :, c0 - side * PIX_HALF : c1 - side * PIX_HALF].rearrange("p t (c i) -> p c t i", i=2),
+                brdf_sb[:, :, c0:c1].rearrange("p t (c i) -> p c t i", i=2),
+                ALU.mult,
+            )
+
+        def mix(g):
+            c0, c1 = PIX_PIECES[g]
+            width = c1 - c0
+            hid_q = tile(f"hid_q{g}", [P, width], U32)
+            hid_s = tile(f"hid_s{g}", [P, width], U8)
+            res = tile(f"res{g}", [P, width], F32)
+            nc.vector.quantize_mx(out=hid_q[:].bitcast(FP8X4), scales=hid_s[:], in_=hid_bf[g][:])
+            acc = psum.tile([P, HALF], F32, name=f"acc{g}", tag=f"bank{g // 2}{g % 2}")
             nc.tensor.matmul_mx(
-                out=acc[:, :PIX_HALF],
+                out=acc[:, :width],
                 lhsT=w2_q[:].bitcast(FP8X4),
                 lhsT_scale=w2_s[:],
-                rhs=hid_q[g][:].bitcast(FP8X4),
-                rhs_scale=hid_s[g][:],
+                rhs=hid_q[:].bitcast(FP8X4),
+                rhs_scale=hid_s[:],
                 start=True,
                 stop=True,
             )
-            nc.scalar.copy(res[g][:], acc[:, :PIX_HALF])
-            nc.sync.dma_start(out=out[:, cols], in_=res[g][:])
+            nc.scalar.copy(res[:], acc[:, :width])
+            nc.sync.dma_start(out=out[:, c0:c1], in_=res[:])
+
+        shade(0)
+        shade(1)
+        mix(0)
+        shade(2)
+        mix(1)
+        mix(2)

@@ -25,7 +25,7 @@ HALF = 512
 HALVES = S // HALF
 PIX_HALF = U // 2
 TINY = 2.0 ** -60
-CAST_SPLIT = 48
+CAST_SPLIT = 64
 PIX_PIECES = ((0, 256), (256, 384), (384, 512))
 
 
@@ -62,7 +62,7 @@ def tile_picked_yphotn_lin_p_kernel(
         nc.sync.dma_start(offs_sb[:], offs)
         nc.gpsimd.memset(xs_sb[:].bitcast(I32), 0)
         for q in range(4):
-            nc.gpsimd.dma_start(
+            nc.sync.dma_start(
                 out=xs_sb[32 * q : 32 * q + 4 * PASSES, :].bitcast(I32),
                 in_=x_scales[:, 4 * q : 4 * q + 4, :].bitcast(I32),
             )
@@ -167,7 +167,7 @@ def tile_picked_yphotn_lin_p_kernel(
 
         lsig = [tile(f"lsig{t}", [P, S], F32) for t in range(PACK)]
         lrad = tile("lrad", [P, PACK * V], F32)
-        est = [tile(f"est{t}", [P, 2 * V], F32) for t in range(PACK)]
+        est = {}
         nflux = [tile(f"nflux{t}", [P, S], F32) for t in range(PACK)]
         fw = [tile(f"fw{t}", [P, 2, S // 2], F32) for t in range(PACK)]
         recip = tile("recip", [P, PACK * V], F32)
@@ -192,6 +192,7 @@ def tile_picked_yphotn_lin_p_kernel(
                     )
 
         def sum_on_tensor(t):
+            est[t] = tile(f"est{t}", [P, 2 * V], F32, f"est{t % 2}")
             turned = psum.tile([P, HALF], F32, name=f"turned{t}", tag=f"bank{t}0")
             for h in range(HALVES):
                 for d in range(D):
@@ -237,11 +238,12 @@ def tile_picked_yphotn_lin_p_kernel(
         weigh(1)
         nums.append(sum_on_tensor(1))
         weigh(2)
-        nums.append(sum_on_tensor(2))
         for t in range(2):
             estimate(t, nums[t], 0, V)
             fetch(t)
+        nums.append(sum_on_tensor(2))
         clamp(LAST)
+        est[LAST] = tile("est_last", [P, 2 * V], F32)
         num_last = est[LAST][:, V:]
         fw_last = fw[LAST][:].rearrange("p e w -> p (e w)")
         for h in range(HALVES):
@@ -257,9 +259,9 @@ def tile_picked_yphotn_lin_p_kernel(
             )
         for h in range(HALVES):
             estimate(LAST, num_last, h * P, (h + 1) * P)
+        nc.vector.tensor_copy(fetched(LAST, 0, PIX_HALF), looked_up(LAST, 0, PIX_HALF))
         estimate(2, nums[2], 0, V)
         fetch(2)
-        nc.vector.tensor_copy(fetched(LAST, 0, PIX_HALF), looked_up(LAST, 0, PIX_HALF))
         nc.vector.tensor_copy(fetched(LAST, PIX_HALF, U), looked_up(LAST, PIX_HALF, U))
 
         hid_bf = [tile(f"hid_bf{c0}", [P, (c1 - c0) * PACK], BF16) for c0, c1 in PIX_PIECES]

@@ -25,7 +25,7 @@ HALF = 512
 HALVES = S // HALF
 PIX_HALF = U // 2
 TINY = 2.0 ** -60
-CAST_SPLIT = 64
+CAST_SPLIT = 40
 PIX_PIECES = ((0, 256), (256, 384), (384, 512))
 
 
@@ -231,9 +231,9 @@ def tile_picked_yphotn_lin_p_kernel(
         nums = []
         weigh(0)
         nums.append(sum_on_tensor(0))
-        for c0 in (0, 2 * V):
+        for c0, c1 in ((0, V), (V, PACK * V)):
             nc.scalar.activation(
-                recip[:, c0 : c0 + 2 * V], lrad[:, c0 : c0 + 2 * V], ACT.Sigmoid, scale=-2.0, bias=-math.log(5.0)
+                recip[:, c0:c1], lrad[:, c0:c1], ACT.Sigmoid, scale=-2.0, bias=-math.log(5.0)
             )
         weigh(1)
         nums.append(sum_on_tensor(1))
@@ -262,7 +262,7 @@ def tile_picked_yphotn_lin_p_kernel(
         nc.vector.tensor_copy(fetched(LAST, 0, PIX_HALF), looked_up(LAST, 0, PIX_HALF))
         estimate(2, nums[2], 0, V)
         fetch(2)
-        nc.vector.tensor_copy(fetched(LAST, PIX_HALF, U), looked_up(LAST, PIX_HALF, U))
+        nc.scalar.activation(fetched(LAST, PIX_HALF, U), looked_up(LAST, PIX_HALF, U), ACT.Copy)
 
         hid_bf = [tile(f"hid_bf{c0}", [P, (c1 - c0) * PACK], BF16) for c0, c1 in PIX_PIECES]
 

import math
from contextlib import ExitStack

import concourse.mybir as mybir
from concourse.masks import make_identity

K, T, S, D, N, H, V, U = 1024, 2048, 1024, 4, 128, 512, 256, 512
FLOPS = 2 * K * H * S + 2 * H * N * U

F32 = mybir.dt.float32
BF16 = mybir.dt.bfloat16
I32 = mybir.dt.int32
U32 = mybir.dt.uint32
U16 = mybir.dt.uint16
U8 = mybir.dt.uint8
FP8X4 = mybir.dt.float8_e4m3fn_x4
ALU = mybir.AluOpType
ACT = mybir.ActivationFunctionType
AX = mybir.AxisListType

P = 128
PACK = 4
PASSES = K // (P * PACK)
HALF = 512
HALVES = S // HALF
PIX_HALF = U // 2
TINY = 2.0 ** -60
CAST_SPLIT = 40
PIX_PIECES = ((0, 256), (256, 384), (384, 512))


def tile_picked_yphotn_lin_p_kernel(
    tc, x_words, x_scales, w1, dist, brdf, unit, w2, offs, pix, out
):
    nc = tc.nc
    with ExitStack() as ctx:
        lists = ctx.enter_context(tc.tile_pool(name="lists", bufs=1))
        sb = ctx.enter_context(tc.tile_pool(name="sb", bufs=1))
        psum = ctx.enter_context(tc.psum_pool(name="psum", bufs=1))

        def tile(name, shape, dtype, tag=None):
            return sb.tile(shape, dtype, name=name, tag=tag or name, align_bytes=64)

        offs_sb = lists.tile([P, S // 16], U16, name="offs_sb")
        pix_sb = lists.tile([P, U // 16], U16, name="pix_sb")

        x_sb = [tile(f"x_sb{o}", [P, T], U32) for o in range(PASSES)]
        xs_sb = tile("xs_sb", [P, T], U8)
        w1_sb = [tile(f"w1_sb{o}", [P, PACK, H], F32) for o in range(PASSES)]
        dist_sb = [tile(f"dist_sb{t}", [P, S], F32) for t in range(PACK)]
        brdf_sb = tile("brdf_sb", [P, PACK, U], F32)
        w2_sb = tile("w2_sb", [P, PACK, N], F32)
        unit_sb = tile("unit_sb", [P, PACK], F32)

        def load_words(o):
            nc.sync.dma_start(
                out=x_sb[o][:].bitcast(I32),
                in_=x_words[o].rearrange("p n t -> p (n t)").bitcast(I32),
            )

        load_words(0)
        nc.sync.dma_start(offs_sb[:], offs)
        nc.gpsimd.memset(xs_sb[:].bitcast(I32), 0)
        for q in range(4):
            nc.sync.dma_start(
                out=xs_sb[32 * q : 32 * q + 4 * PASSES, :].bitcast(I32),
                in_=x_scales[:, 4 * q : 4 * q + 4, :].bitcast(I32),
            )
        for o in range(PASSES):
            nc.sync.dma_start(
                out=w1_sb[o][:],
                in_=w1[512 * o : 512 * (o + 1), :].rearrange("(p j) c -> p j c", j=PACK),
            )
        load_words(1)
        dist_rows = dist.rearrange("(p t) s -> p t s", t=PACK)
        for t in range(PACK):
            nc.sync.dma_start(out=dist_sb[t][:], in_=dist_rows[:, t, :])
        nc.sync.dma_start(out=w2_sb[:], in_=w2.rearrange("(p t) n -> p t n", t=PACK))
        nc.sync.dma_start(out=unit_sb[:], in_=unit.rearrange("(p t) o -> p (t o)", t=PACK))
        nc.sync.dma_start(pix_sb[:], pix)
        nc.sync.dma_start(out=brdf_sb[:], in_=brdf.rearrange("(p t) r -> p t r", t=PACK))

        ident = tile("ident", [P, P], F32)
        make_identity(nc, ident[:])
        warm = tile("warm", [P, 2], F32)
        nc.vector.memset(warm[:, 0:1], 0.0)
        nc.scalar.activation(warm[:, 1:2], warm[:, 0:1], ACT.Sigmoid)

        xg = {}
        sg = [tile(f"sg{h}", [P, HALF], U8) for h in range(HALVES)]
        w1_bf = [tile(f"w1_bf{o}", [P, PACK * H], BF16) for o in range(PASSES)]
        w1_q = [tile(f"w1_q{o}", [P, H], U32) for o in range(PASSES)]
        w1_s = [tile(f"w1_s{o}", [P, H], U8) for o in range(PASSES)]

        def offs_half(h):
            return offs_sb[:, h * (HALF // 16) : (h + 1) * (HALF // 16)]

        def gather_words(o, h, tag=None):
            xg[o, h] = tile(f"xg{o}{h}", [P, HALF], U32, tag)
            nc.vector.tensor_copy(xg[o, h][:], x_sb[o][:].indirect(offs_half(h)))

        def gather_scales(h):
            nc.vector.tensor_copy(sg[h][:], xs_sb[:].indirect(offs_half(h)))

        def w1_views(o, m0, m1):
            dst = w1_bf[o][:].rearrange("p (t m j) -> p m t j", t=PACK, j=PACK)[:, m0:m1]
            src = w1_sb[o][:].rearrange("p j (m t) -> p m t j", t=PACK)[:, m0:m1]
            return dst, src

        def quantize_w1(o):
            nc.vector.quantize_mx(out=w1_q[o][:].bitcast(FP8X4), scales=w1_s[o][:], in_=w1_bf[o][:])

        for h in range(HALVES):
            gather_words(0, h)
        dst, src = w1_views(0, 0, P)
        nc.scalar.copy(dst, src)
        for h in range(HALVES):
            gather_scales(h)
        dst, src = w1_views(1, 0, CAST_SPLIT)
        nc.scalar.copy(dst, src)
        dst, src = w1_views(1, CAST_SPLIT, P)
        nc.vector.tensor_copy(dst, src)
        quantize_w1(0)
        quantize_w1(1)
        gather_words(1, 0, "xs_sb")
        gather_words(1, 1)

        y = [[psum.tile([P, HALF], F32, name=f"y{t}{h}", tag=f"bank{t}{h}") for h in range(HALVES)] for t in range(PACK)]
        sig = [tile(f"sig{t}", [P, S], F32) for t in range(PACK)]

        def half(tl, h):
            return tl[:, h * HALF : (h + 1) * HALF]

        for h in range(HALVES):
            for t in range(PACK):
                cols = slice(P * t, P * (t + 1))
                for o in range(PASSES):
                    nc.tensor.matmul_mx(
                        out=y[t][h][:],
                        lhsT=w1_q[o][:, cols].bitcast(FP8X4),
                        lhsT_scale=w1_s[o][:, cols],
                        rhs=xg[o, h][:].bitcast(FP8X4),
                        rhs_scale=sg[h][4 * o : P, :],
                        start=(o == 0),
                        stop=(o == PASSES - 1),
                    )
                nc.scalar.activation(half(sig[t], h), y[t][h][:], ACT.Sigmoid, scale=-1.0)

        rad = tile("rad", [P, PACK, V], F32, "x_sb1")
        arad = tile("arad", [P, PACK * V], F32)
        ncone = [tile(f"ncone{t}", [P, S], F32) for t in range(PACK)]
        for t in range(PACK):
            nc.vector.tensor_reduce(rad[:, t, :], dist_sb[t][:].rearrange("p (v d) -> p v d", d=D), AX.X, ALU.max)
            nc.gpsimd.tensor_scalar(ncone[t][:], dist_sb[t][:], -1.0, 1.0, ALU.mult, ALU.add)
        rad_flat = rad[:].rearrange("p t v -> p (t v)")
        nc.vector.scalar_tensor_tensor(arad[:], rad_flat, -1.0, rad_flat, ALU.mult, ALU.max)
        w2_bf = tile("w2_bf", [P, N * PACK], BF16)
        w2_q = tile("w2_q", [P, N], U32)
        w2_s = tile("w2_s", [P, N], U8)
        nc.vector.tensor_copy(
            w2_bf[:].rearrange("p (c i t) -> p c t i", i=2, t=PACK),
            w2_sb[:].rearrange("p t (c i) -> p c t i", i=2),
        )
        nc.vector.quantize_mx(out=w2_q[:].bitcast(FP8X4), scales=w2_s[:], in_=w2_bf[:])
        unit5 = tile("unit5", [P, PACK], F32)
        nc.gpsimd.tensor_scalar(unit5[:], unit_sb[:], -5.0, 0.0, ALU.mult, ALU.add)

        lsig = [tile(f"lsig{t}", [P, S], F32) for t in range(PACK)]
        lrad = tile("lrad", [P, PACK * V], F32)
        est = {}
        nflux = [tile(f"nflux{t}", [P, S], F32) for t in range(PACK)]
        fw = [tile(f"fw{t}", [P, 2, S // 2], F32) for t in range(PACK)]
        recip = tile("recip", [P, PACK * V], F32)
        ep = [tile(f"ep{g}", [P, PACK, PIX_HALF], F32) for g in range(2)]
        LAST = PACK - 1

        def clamp(t):
            for h in range(HALVES):
                nc.vector.scalar_tensor_tensor(half(nflux[t], h), y[t][h][:], -1.0, half(lsig[t], h), ALU.mult, ALU.min)

        def weigh(t):
            clamp(t)
            for h in range(HALVES):
                for e in range(2):
                    nc.vector.scalar_tensor_tensor(
                        fw[t][:, e, 2 * P * h : 2 * P * (h + 1)].rearrange("p (v d) -> p v d", d=2),
                        half(ncone[t], h).rearrange("p (v e d) -> p v e d", e=2, d=2)[:, :, e, :],
                        0.0,
                        half(nflux[t], h).rearrange("p (v e d) -> p v e d", e=2, d=2)[:, :, e, :],
                        ALU.max,
                        ALU.mult,
                    )

        def sum_on_tensor(t):
            est[t] = tile(f"est{t}", [P, 2 * V], F32, f"est{t % 2}")
            turned = psum.tile([P, HALF], F32, name=f"turned{t}", tag=f"bank{t}0")
            for h in range(HALVES):
                for d in range(D):
                    c0 = 2 * P * h + d % 2
                    nc.tensor.matmul(
                        turned[:, h * P : (h + 1) * P], fw[t][:, d // 2, c0 : 2 * P * (h + 1) : 2], ident[:],
                        start=(d == 0), stop=(d == D - 1), is_transpose=True,
                    )
            nc.scalar.copy(est[t][:, V:], turned[:, :V])
            back = psum.tile([P, HALF], F32, name=f"back{t}", tag=f"bank{t}1")
            for h in range(HALVES):
                nc.tensor.transpose(back[:, h * P : (h + 1) * P], est[t][:, V + h * P : V + (h + 1) * P], ident[:])
            return back[:, :V]

        def estimate(t, num, c0, c1):
            nc.vector.scalar_tensor_tensor(
                est[t][:, c0:c1], num[:, c0:c1], unit5[:, t : t + 1], recip[:, t * V + c0 : t * V + c1], ALU.mult, ALU.mult
            )

        def looked_up(t, c0, c1):
            return est[t][:].indirect(pix_sb[:, c0 // 16 : c1 // 16])

        def fetched(t, c0, c1):
            g = c0 // PIX_HALF
            return ep[g][:, t, c0 - g * PIX_HALF : c1 - g * PIX_HALF]

        def fetch(t):
            for c0 in (0, PIX_HALF):
                nc.scalar.activation(fetched(t, c0, c0 + PIX_HALF), looked_up(t, c0, c0 + PIX_HALF), ACT.Copy)

        for h in range(HALVES):
            nc.scalar.activation(half(lsig[0], h), half(sig[0], h), ACT.Ln, bias=TINY)
        for t in range(1, PACK):
            nc.scalar.activation(lsig[t][:], sig[t][:], ACT.Ln, bias=TINY)
        nc.scalar.activation(lrad[:], arad[:], ACT.Ln, bias=TINY)
        nums = []
        weigh(0)
        nums.append(sum_on_tensor(0))
        for c0, c1 in ((0, V), (V, PACK * V)):
            nc.scalar.activation(
                recip[:, c0:c1], lrad[:, c0:c1], ACT.Sigmoid, scale=-2.0, bias=-math.log(5.0)
            )
        weigh(1)
        nums.append(sum_on_tensor(1))
        weigh(2)
        for t in range(2):
            estimate(t, nums[t], 0, V)
            fetch(t)
        nums.append(sum_on_tensor(2))
        clamp(LAST)
        est[LAST] = tile("est_last", [P, 2 * V], F32)
        num_last = est[LAST][:, V:]
        fw_last = fw[LAST][:].rearrange("p e w -> p (e w)")
        for h in range(HALVES):
            nc.vector.scalar_tensor_tensor(
                fw_last[:, h * HALF : (h + 1) * HALF], half(ncone[LAST], h), 0.0, half(nflux[LAST], h), ALU.max, ALU.mult
            )
        for h in range(HALVES):
            nc.vector.tensor_reduce(
                num_last[:, h * P : (h + 1) * P],
                fw_last[:, h * HALF : (h + 1) * HALF].rearrange("p (v d) -> p v d", d=D),
                AX.X,
                ALU.add,
            )
        for h in range(HALVES):
            estimate(LAST, num_last, h * P, (h + 1) * P)
        nc.vector.tensor_copy(fetched(LAST, 0, PIX_HALF), looked_up(LAST, 0, PIX_HALF))
        estimate(2, nums[2], 0, V)
        fetch(2)
        nc.scalar.activation(fetched(LAST, PIX_HALF, U), looked_up(LAST, PIX_HALF, U), ACT.Copy)

        hid_bf = [tile(f"hid_bf{c0}", [P, (c1 - c0) * PACK], BF16) for c0, c1 in PIX_PIECES]

        def shade(g):
            c0, c1 = PIX_PIECES[g]
            side = c0 // PIX_HALF
            nc.vector.tensor_tensor(
                hid_bf[g][:].rearrange("p (c i t) -> p c t i", i=2, t=PACK),
                ep[side][:, :, c0 - side * PIX_HALF : c1 - side * PIX_HALF].rearrange("p t (c i) -> p c t i", i=2),
                brdf_sb[:, :, c0:c1].rearrange("p t (c i) -> p c t i", i=2),
                ALU.mult,
            )

        def mix(g):
            c0, c1 = PIX_PIECES[g]
            width = c1 - c0
            hid_q = tile(f"hid_q{g}", [P, width], U32)
            hid_s = tile(f"hid_s{g}", [P, width], U8)
            res = tile(f"res{g}", [P, width], F32)
            nc.vector.quantize_mx(out=hid_q[:].bitcast(FP8X4), scales=hid_s[:], in_=hid_bf[g][:])
            acc = psum.tile([P, HALF], F32, name=f"acc{g}", tag=f"bank{g // 2}{g % 2}")
            nc.tensor.matmul_mx(
                out=acc[:, :width],
                lhsT=w2_q[:].bitcast(FP8X4),
                lhsT_scale=w2_s[:],
                rhs=hid_q[:].bitcast(FP8X4),
                rhs_scale=hid_s[:],
                start=True,
                stop=True,
            )
            nc.scalar.copy(res[:], acc[:, :width])
            nc.sync.dma_start(out=out[:, c0:c1], in_=res[:])

        shade(0)
        shade(1)
        mix(0)
        shade(2)
        mix(1)
        mix(2)
